import numpy as np
import ml_dtypes


def mxq(x, axis, fmt="e4m3"):
    dtype, down = {"e4m3": (ml_dtypes.float8_e4m3fn, 7), "e5m2": (ml_dtypes.float8_e5m2, 14)}[fmt]
    v = np.moveaxis(np.asarray(x, np.float32).astype(ml_dtypes.bfloat16).astype(np.float64), axis, -1)
    blocks = v.reshape(v.shape[:-1] + (-1, 32))
    amax = np.abs(blocks).max(-1, keepdims=True)
    byte = np.maximum(np.where(amax > 0, np.frexp(amax)[1] - 1 + 127, 0) - down, 1)
    scale = np.exp2(byte - 127.0)
    codes = (blocks / scale).astype(np.float32).astype(dtype).astype(np.float64)
    return np.moveaxis((codes * scale).reshape(v.shape), -1, axis)


WIDE = False


def mx_kscale(k, group=512):
    if not WIDE:
        return np.ones(k)
    levels = np.array([18, -18])
    if group != 512:
        return np.exp2(np.random.permutation(np.resize(levels, k // group))).repeat(group)
    if k % 512:
        return np.exp2(np.random.permutation(np.resize(levels, k // 32))).repeat(32)
    a = np.empty((k // 512, 16))
    for p in range(k // 512):
        a[p, :8] = np.random.permutation(np.resize(levels, 8))
        for g in range(8):
            far = levels[np.abs(levels - a[p, g]) >= 10]
            a[p, g + 8] = far[np.random.randint(len(far))]
    return np.exp2(a.ravel()).repeat(32)


def f64(x):
    return np.asarray(x).astype(np.float64)


H, D, N = 8, 128, 512


def setup_inputs():
    n = np.random.standard_normal
    s = mx_kscale(D, 0)
    u = mx_kscale(N)
    t = np.random.uniform(0.5, 2.0, N) * u
    v = n((H, N, 128))
    return {
        "q": n((H, D, N)).astype(np.float32),
        "qa": (np.random.uniform(0.5, 2.0, D) * s)[:, None].astype(np.float32),
        "ka": np.tile(np.random.uniform(0.5, 2.0, D) / s, (128, 1)).astype(np.float32),
        "k": n((H, N, D)).astype(np.float32),
        "t": t.reshape(N, 1).astype(np.float32),
        "v": (v / t[:, None]).astype(np.float32),
    }


def reference(q, qa, ka, k, t, v):
    fq = (np.square(f64(q)) + 0.125) * f64(qa)
    fk = (np.square(f64(k)) + 0.125) * f64(t) * f64(ka)[:1]
    S = (mxq(fk, 1, "e4m3").transpose(0, 2, 1) @ mxq(f64(v), 1, "e4m3")) / N
    y = mxq(fq, 1, "e4m3").transpose(0, 2, 1) @ mxq(S, 1, "e4m3")
    return y

@@ -1,0 +1,346 @@
+from contextlib import ExitStack
+
+import concourse.mybir as mybir
+
+H, D, N = 8, 128, 512
+FLOPS = 2 * 2 * H * N * D * 128
+
+F32 = mybir.dt.float32
+BF16 = mybir.dt.bfloat16
+U32 = mybir.dt.uint32
+I32 = mybir.dt.int32
+U8 = mybir.dt.uint8
+FP8X4 = mybir.dt.float8_e4m3fn_x4
+ACT = mybir.ActivationFunctionType
+ALU = mybir.AluOpType
+
+P = 128
+
+
+def tile_rows_lin_sq_kernel(tc, q, qa, ka, k, t, v, out):
+    nc = tc.nc
+    with ExitStack() as ctx:
+        sb = ctx.enter_context(tc.tile_pool(name="sb", bufs=1))
+        ps = ctx.enter_context(tc.psum_pool(name="ps", bufs=1))
+        ctx.enter_context(tc.manual_schedule())
+
+        def tiles(name, count, shape, dtype):
+            return [sb.tile(shape, dtype, name="%s%d" % (name, i), align_bytes=64) for i in range(count)]
+
+        ka_sb = sb.tile([P, D], F32, name="ka_sb")
+        t_sb = sb.tile([P, 4], F32, name="t_sb")
+        qa_sb = sb.tile([P, 4], F32, name="qa_sb")
+        w = sb.tile([P, 512], F32, name="w")
+        k_raw = {}
+        v_raw = {}
+        q_raw = {}
+        k_sq = tiles("k_sq", 8, [P, 512], F32)
+        k_bf = tiles("k_bf", 4, [P, 4, 2, 128], BF16)
+        k_codes = tiles("k_codes", 4, [P, 256], U32)
+        k_scales = tiles("k_scales", 4, [P, 384], U8)
+        k_pad = tiles("k_pad", 2, [P, 1152], U32)
+        v_bf = tiles("v_bf", 4, [P, 2, 128, 4], BF16)
+        v_codes = tiles("v_codes", 4, [P, 256], U32)
+        v_scales = tiles("v_scales", 4, [P, 256], U8)
+        q_sq = tiles("q_sq", 4, [P, 256, 4], F32)
+        q_bf = tiles("q_bf", 4, [P, 2, 128, 4], BF16)
+        q_codes = tiles("q_codes", 4, [P, 256], U32)
+        q_scales = tiles("q_scales", 4, [P, 256], U8)
+        s_bf = tiles("s_bf", 2, [P, 128, 4], BF16)
+        s_codes = tiles("s_codes", 2, [P, 128], U32)
+        s_scales = tiles("s_scales", 2, [P, 128], U8)
+        y_sb = tiles("y_sb", 8, [P, 2, 256], F32)
+        s_bank = [ps.tile([P, 512], F32, name="s_bank%d" % i) for i in range(2)]
+        y_bank = [ps.tile([P, 512], F32, name="y_bank%d" % i) for i in range(4)]
+
+        def load_small():
+            nc.scalar.dma_start(out=ka_sb[:], in_=ka)
+            nc.scalar.dma_start(out=t_sb[:], in_=t.rearrange("(p j) o -> p (j o)", j=4))
+            nc.scalar.dma_start(
+                out=qa_sb[:],
+                in_=qa.rearrange("(o p j) z -> o p (j z)", o=1, j=4).to_broadcast([4, 32, 4]),
+            )
+
+        def load_rows(src, store, name, h0, count):
+            raw = sb.tile([P, count, 4, 128], F32, name="%s%d" % (name, h0))
+            nc.sync.dma_start(
+                out=raw[:].rearrange("p h j d -> p h (j d)"),
+                in_=src[h0 : h0 + count].rearrange("h (p j) d -> p h (j d)", j=4),
+            )
+            for i in range(count):
+                store[h0 + i] = (raw, i)
+
+        def LK(h0, count):
+            load_rows(k, k_raw, "k_raw", h0, count)
+
+        def LV(h0, count):
+            load_rows(v, v_raw, "v_raw", h0, count)
+
+        def LQ(s):
+            raw = sb.tile([P, 4, 512], F32, name="q_raw%d" % s)
+            nc.sync.dma_start(out=raw[:], in_=q[4 * s : 4 * s + 4].rearrange("c (p j) n -> (c p) j n", j=4))
+            for u in range(2):
+                q_raw[2 * s + u] = raw[:, :, 256 * u : 256 * u + 256]
+
+        def LQH(s, u):
+            raw = sb.tile([P, 4, 256], F32, name="q_rawh%d" % (2 * s + u))
+            nc.sync.dma_start(
+                out=raw[:],
+                in_=q[4 * s : 4 * s + 4].rearrange("c (p j) n -> (c p) j n", j=4)[:, :, 256 * u : 256 * u + 256],
+            )
+            q_raw[2 * s + u] = raw[:]
+
+        def ZERO():
+            for g in range(2):
+                nc.vector.memset(k_pad[g][:], 0)
+            for g in range(4):
+                nc.vector.memset(k_scales[g][:].bitcast(U32), 0)
+
+        def W():
+            nc.vector.tensor_tensor(
+                out=w[:].rearrange("p (x m j) -> p x m j", x=4, j=4),
+                in0=ka_sb[:].rearrange("p (m x) -> p x m", x=4).unsqueeze(3).to_broadcast([P, 4, 32, 4]),
+                in1=t_sb[:].unsqueeze(1).unsqueeze(1).to_broadcast([P, 4, 32, 4]),
+                op=ALU.mult,
+            )
+
+        def SK(h):
+            raw, i = k_raw[h]
+            nc.scalar.activation(
+                out=k_sq[h][:].rearrange("p (x m j) -> p m j x", x=4, j=4),
+                in_=raw[:, i].rearrange("p j (m x) -> p m j x", x=4),
+                func=ACT.Square,
+            )
+
+        def TK(h):
+            nc.vector.scalar_tensor_tensor(
+                out=k_bf[h // 2][:, :, h % 2, :],
+                in0=k_sq[h][:].rearrange("p (x r) -> p x r", x=4),
+                scalar=0.125,
+                in1=w[:].rearrange("p (x r) -> p x r", x=4),
+                op0=ALU.add,
+                op1=ALU.mult,
+            )
+
+        def QK(g):
+            nc.vector.quantize_mx(
+                out=k_codes[g][:].bitcast(FP8X4),
+                scales=k_scales[g][:, 64:320],
+                in_=k_bf[g][:].rearrange("p x c r -> p (x c r)"),
+            )
+
+        def CK(g):
+            base = 64 * (g % 2)
+            dst = k_pad[g % 2][:, base : base + 1088].bitcast(I32).rearrange("p (c r) -> p c r", c=2)
+            dst = dst[:, :, 0:512].rearrange("p c (x m) -> p c x m", x=4)[:, :, :, 0:32]
+            nc.vector.tensor_copy(
+                out=dst, in_=k_codes[g][:].bitcast(I32).rearrange("p (x c m) -> p c x m", x=4, c=2)
+            )
+
+        def cv_views(g):
+            raw, i = v_raw[2 * g]
+            return (
+                v_bf[g][:].rearrange("p h (c i) j -> p h c j i", i=4),
+                raw[:].rearrange("p h j (c i) -> p h c j i", i=4),
+            )
+
+        def CV(g):
+            dst, src = cv_views(g)
+            nc.vector.tensor_copy(out=dst, in_=src)
+
+        def CVA(g):
+            dst, src = cv_views(g)
+            nc.scalar.copy(out=dst, in_=src)
+
+        def QV(g):
+            nc.vector.quantize_mx(
+                out=v_codes[g][:].bitcast(FP8X4),
+                scales=v_scales[g][:],
+                in_=v_bf[g][:].rearrange("p h e j -> p (h e j)"),
+            )
+
+        def MS(s):
+            for x in range(4):
+                for c in range(4):
+                    g = 2 * s + c // 2
+                    col = 512 * (c % 2) + 128 * x
+                    sc = 64 + 64 * x - 64 * (c // 2)
+                    e0 = 128 * (c % 2)
+                    nc.tensor.matmul_mx(
+                        out=s_bank[s][:, 128 * x : 128 * x + 128],
+                        lhsT=k_pad[c // 2][:, col : col + 128].bitcast(FP8X4),
+                        lhsT_scale=k_scales[g][:, sc : sc + 128],
+                        rhs=v_codes[g][:, e0 : e0 + 128].bitcast(FP8X4),
+                        rhs_scale=v_scales[g][:, e0 : e0 + 128],
+                        start=(c == 0),
+                        stop=(c == 3),
+                    )
+
+        def ES(s):
+            nc.scalar.activation(
+                out=s_bf[s][:],
+                in_=s_bank[s][:].rearrange("p (x e) -> p e x", x=4),
+                func=ACT.Copy,
+                scale=1.0 / N,
+            )
+
+        def QS(s):
+            nc.vector.quantize_mx(
+                out=s_codes[s][:].bitcast(FP8X4),
+                scales=s_scales[s][:],
+                in_=s_bf[s][:].rearrange("p e x -> p (e x)"),
+            )
+
+        def SQ(s, u):
+            nc.scalar.activation(
+                out=q_sq[2 * s + u][:].rearrange("p (c i) j -> p c j i", i=4),
+                in_=q_raw[2 * s + u].rearrange("p j (c i) -> p c j i", i=4),
+                func=ACT.Square,
+            )
+
+        def TQ(s, u, r):
+            nc.vector.scalar_tensor_tensor(
+                out=q_bf[2 * s + u][:, r],
+                in0=q_sq[2 * s + u][:].rearrange("p (m r) j -> p r m j", r=2)[:, r],
+                scalar=0.125,
+                in1=qa_sb[:].unsqueeze(1).to_broadcast([P, 128, 4]),
+                op0=ALU.add,
+                op1=ALU.mult,
+            )
+
+        def QQ(s, u):
+            nc.vector.quantize_mx(
+                out=q_codes[2 * s + u][:].bitcast(FP8X4),
+                scales=q_scales[2 * s + u][:],
+                in_=q_bf[2 * s + u][:].rearrange("p r m j -> p (r m j)"),
+            )
+
+        def MY(s, u):
+            for r in range(2):
+                for c in range(4):
+                    rows = slice(32 * c, 32 * c + 32)
+                    cols = slice(128 * r, 128 * r + 128)
+                    o = 256 * u + 128 * r
+                    nc.tensor.matmul_mx(
+                        out=y_bank[c][:, o : o + 128],
+                        lhsT=q_codes[2 * s + u][rows, cols].bitcast(FP8X4),
+                        lhsT_scale=q_scales[2 * s + u][rows, cols],
+                        rhs=s_codes[s][rows, :].bitcast(FP8X4),
+                        rhs_scale=s_scales[s][rows, :],
+                        start=True,
+                        stop=True,
+                    )
+
+        def EA(s, u, c):
+            nc.scalar.copy(out=y_sb[4 * s + 2 * u + c // 2][:, c % 2, :], in_=y_bank[c][:, 256 * u : 256 * u + 256])
+
+        def EV(s, u, c):
+            nc.vector.tensor_copy(
+                out=y_sb[4 * s + 2 * u + c // 2][:, c % 2, :], in_=y_bank[c][:, 256 * u : 256 * u + 256]
+            )
+
+        def ST(s, u, g):
+            h0 = 4 * s + 2 * g
+            nc.sync.dma_start(
+                out=out[h0 : h0 + 2, 256 * u : 256 * u + 256, :].rearrange("c (p r) e -> p c (r e)", r=2),
+                in_=y_sb[4 * s + 2 * u + g][:],
+            )
+
+        load_small()
+        LK(0,1)
+        LK(1,1)
+        LK(2,2)
+        LQH(0,0)
+        LQH(0,1)
+        LV(0,2)
+        LV(2,2)
+        LK(4,2)
+        LK(6,2)
+        LV(4,2)
+        LV(6,2)
+        LQH(1,0)
+        LQH(1,1)
+        ZERO()
+        W()
+        SK(0)
+        TK(0)
+        SK(1)
+        TK(1)
+        SK(2)
+        TK(2)
+        QK(0)
+        SK(3)
+        TK(3)
+        CK(0)
+        SQ(0,0)
+        QK(1)
+        TQ(0,0,0)
+        CK(1)
+        TQ(0,0,1)
+        SQ(0,1)
+        CVA(0)
+        CVA(1)
+        TQ(0,1,0)
+        QQ(0,0)
+        TQ(0,1,1)
+        QV(0)
+        QQ(0,1)
+        QV(1)
+        MS(0)
+        SK(4)
+        SK(5)
+        TK(4)
+        TK(5)
+        SK(6)
+        ES(0)
+        SK(7)
+        QK(2)
+        TK(6)
+        QS(0)
+        TK(7)
+        CK(2)
+        CV(2)
+        QK(3)
+        QV(2)
+        CK(3)
+        CV(3)
+        MY(0,0)
+        EA(0,0,0)
+        EA(0,0,1)
+        ST(0,0,0)
+        EA(0,0,2)
+        EA(0,0,3)
+        ST(0,0,1)
+        MY(0,1)
+        SQ(1,0)
+        QV(3)
+        MS(1)
+        TQ(1,0,0)
+        TQ(1,0,1)
+        EA(0,1,0)
+        EA(0,1,1)
+        ST(0,1,0)
+        SQ(1,1)
+        ES(1)
+        QQ(1,0)
+        TQ(1,1,0)
+        QS(1)
+        TQ(1,1,1)
+        EA(0,1,2)
+        EA(0,1,3)
+        ST(0,1,1)
+        MY(1,0)
+        QQ(1,1)
+        EA(1,0,0)
+        EA(1,0,1)
+        ST(1,0,0)
+        EV(1,0,2)
+        EV(1,0,3)
+        ST(1,0,1)
+        MY(1,1)
+        EA(1,1,0)
+        EA(1,1,1)
+        ST(1,1,0)
+        EV(1,1,2)
+        EV(1,1,3)
+        ST(1,1,1)

@@ -30,6 +30,7 @@ def tile_rows_lin_sq_kernel(tc, q, qa, ka, k, t, v, out):
         ka_sb = sb.tile([P, D], F32, name="ka_sb")
         t_sb = sb.tile([P, 4], F32, name="t_sb")
         qa_sb = sb.tile([P, 4], F32, name="qa_sb")
+        qa_rep = sb.tile([P, 128], F32, name="qa_rep")
         w = sb.tile([P, 512], F32, name="w")
         k_raw = {}
         v_raw = {}
@@ -38,19 +39,20 @@ def tile_rows_lin_sq_kernel(tc, q, qa, ka, k, t, v, out):
         k_bf = tiles("k_bf", 4, [P, 4, 2, 128], BF16)
         k_codes = tiles("k_codes", 4, [P, 256], U32)
         k_scales = tiles("k_scales", 4, [P, 384], U8)
-        k_pad = tiles("k_pad", 2, [P, 1152], U32)
+        k_pad = tiles("k_pad", 4, [P, 1152], U32)
         v_bf = tiles("v_bf", 4, [P, 2, 128, 4], BF16)
         v_codes = tiles("v_codes", 4, [P, 256], U32)
         v_scales = tiles("v_scales", 4, [P, 256], U8)
-        q_sq = tiles("q_sq", 4, [P, 256, 4], F32)
-        q_bf = tiles("q_bf", 4, [P, 2, 128, 4], BF16)
+        q_sq = tiles("q_sq", 8, [P, 4, 128], F32)
+        q_bf = tiles("q_bf", 2, [P, 4, 512], BF16)
         q_codes = tiles("q_codes", 4, [P, 256], U32)
         q_scales = tiles("q_scales", 4, [P, 256], U8)
         s_bf = tiles("s_bf", 2, [P, 128, 4], BF16)
-        s_codes = tiles("s_codes", 2, [P, 128], U32)
-        s_scales = tiles("s_scales", 2, [P, 128], U8)
-        y_sb = tiles("y_sb", 8, [P, 2, 256], F32)
-        s_bank = [ps.tile([P, 512], F32, name="s_bank%d" % i) for i in range(2)]
+        s_codes = tiles("s_codes", 4, [P, 128], U32)
+        s_scales = tiles("s_scales", 4, [P, 128], U8)
+        y_sb = tiles("y_sb", 8, [P, 512], F32)
+        s_bank = [ps.tile([P, 512], F32, name="s_bank%d" % i) for i in range(4)]
+        s_of = {}
         y_bank = [ps.tile([P, 512], F32, name="y_bank%d" % i) for i in range(4)]
 
         def load_small():
@@ -79,8 +81,7 @@ def tile_rows_lin_sq_kernel(tc, q, qa, ka, k, t, v, out):
         def LQ(s):
             raw = sb.tile([P, 4, 512], F32, name="q_raw%d" % s)
             nc.sync.dma_start(out=raw[:], in_=q[4 * s : 4 * s + 4].rearrange("c (p j) n -> (c p) j n", j=4))
-            for u in range(2):
-                q_raw[2 * s + u] = raw[:, :, 256 * u : 256 * u + 256]
+            q_raw[s] = raw
 
         def LQH(s, u):
             raw = sb.tile([P, 4, 256], F32, name="q_rawh%d" % (2 * s + u))
@@ -91,10 +92,10 @@ def tile_rows_lin_sq_kernel(tc, q, qa, ka, k, t, v, out):
             q_raw[2 * s + u] = raw[:]
 
         def ZERO():
-            for g in range(2):
-                nc.vector.memset(k_pad[g][:], 0)
             for g in range(4):
-                nc.vector.memset(k_scales[g][:].bitcast(U32), 0)
+                nc.gpsimd.memset(k_pad[g][:], 0)
+            for g in range(4):
+                nc.gpsimd.memset(k_scales[g][:].bitcast(U32), 0)
 
         def W():
             nc.vector.tensor_tensor(
@@ -102,6 +103,13 @@ def tile_rows_lin_sq_kernel(tc, q, qa, ka, k, t, v, out):
                 in0=ka_sb[:].rearrange("p (m x) -> p x m", x=4).unsqueeze(3).to_broadcast([P, 4, 32, 4]),
                 in1=t_sb[:].unsqueeze(1).unsqueeze(1).to_broadcast([P, 4, 32, 4]),
                 op=ALU.mult,
+            )
+
+
+        def QA():
+            nc.vector.tensor_copy(
+                out=qa_rep[:].rearrange("p (m j) -> p m j", j=4),
+                in_=qa_sb[:].unsqueeze(1).to_broadcast([P, 32, 4]),
             )
 
         def SK(h):
@@ -131,216 +139,237 @@ def tile_rows_lin_sq_kernel(tc, q, qa, ka, k, t, v, out):
 
         def CK(g):
             base = 64 * (g % 2)
-            dst = k_pad[g % 2][:, base : base + 1088].bitcast(I32).rearrange("p (c r) -> p c r", c=2)
+            dst = k_pad[g][:, base : base + 1088].bitcast(I32).rearrange("p (c r) -> p c r", c=2)
             dst = dst[:, :, 0:512].rearrange("p c (x m) -> p c x m", x=4)[:, :, :, 0:32]
             nc.vector.tensor_copy(
                 out=dst, in_=k_codes[g][:].bitcast(I32).rearrange("p (x c m) -> p c x m", x=4, c=2)
             )
 
-        def cv_views(g):
-            raw, i = v_raw[2 * g]
+        def ch_views(h):
+            raw, i = v_raw[h]
             return (
-                v_bf[g][:].rearrange("p h (c i) j -> p h c j i", i=4),
-                raw[:].rearrange("p h j (c i) -> p h c j i", i=4),
+                v_bf[h // 2][:, h % 2].rearrange("p (c i) j -> p c j i", i=4),
+                raw[:, i].rearrange("p j (c i) -> p c j i", i=4),
             )
 
-        def CV(g):
-            dst, src = cv_views(g)
+        def CH(h):
+            dst, src = ch_views(h)
             nc.vector.tensor_copy(out=dst, in_=src)
 
-        def CVA(g):
-            dst, src = cv_views(g)
+        def CHA(h):
+            dst, src = ch_views(h)
             nc.scalar.copy(out=dst, in_=src)
 
-        def QV(g):
+        def QW(g):
             nc.vector.quantize_mx(
                 out=v_codes[g][:].bitcast(FP8X4),
                 scales=v_scales[g][:],
                 in_=v_bf[g][:].rearrange("p h e j -> p (h e j)"),
             )
 
-        def MS(s):
+        def state_passes(bank, heads):
             for x in range(4):
-                for c in range(4):
-                    g = 2 * s + c // 2
-                    col = 512 * (c % 2) + 128 * x
+                for h in heads:
+                    g, c = h // 2, h % 4
+                    col = 512 * (h % 2) + 128 * x
                     sc = 64 + 64 * x - 64 * (c // 2)
-                    e0 = 128 * (c % 2)
+                    e0 = 128 * (h % 2)
                     nc.tensor.matmul_mx(
-                        out=s_bank[s][:, 128 * x : 128 * x + 128],
-                        lhsT=k_pad[c // 2][:, col : col + 128].bitcast(FP8X4),
+                        out=bank[:, 128 * x : 128 * x + 128],
+                        lhsT=k_pad[g][:, col : col + 128].bitcast(FP8X4),
                         lhsT_scale=k_scales[g][:, sc : sc + 128],
                         rhs=v_codes[g][:, e0 : e0 + 128].bitcast(FP8X4),
                         rhs_scale=v_scales[g][:, e0 : e0 + 128],
-                        start=(c == 0),
-                        stop=(c == 3),
+                        start=(h == heads[0]),
+                        stop=(h == heads[-1]),
                     )
 
-        def ES(s):
+        def state_out(bank, s, rows):
             nc.scalar.activation(
-                out=s_bf[s][:],
-                in_=s_bank[s][:].rearrange("p (x e) -> p e x", x=4),
+                out=s_bf[s][rows],
+                in_=bank[rows, :].rearrange("p (x e) -> p e x", x=4),
                 func=ACT.Copy,
                 scale=1.0 / N,
             )
 
-        def QS(s):
+        def state_quant(s, i, rows):
             nc.vector.quantize_mx(
-                out=s_codes[s][:].bitcast(FP8X4),
-                scales=s_scales[s][:],
-                in_=s_bf[s][:].rearrange("p e x -> p (e x)"),
+                out=s_codes[i][rows, :].bitcast(FP8X4),
+                scales=s_scales[i][rows, :],
+                in_=s_bf[s][rows].rearrange("p e x -> p (e x)"),
             )
 
-        def SQ(s, u):
+        def MS(s):
+            state_passes(s_bank[2 * s], [4 * s, 4 * s + 1, 4 * s + 2, 4 * s + 3])
+
+        def ES(s):
+            state_out(s_bank[2 * s], s, slice(0, 128))
+
+        def QS(s):
+            state_quant(s, 2 * s, slice(0, 128))
+            s_of[2 * s] = 2 * s
+            s_of[2 * s + 1] = 2 * s
+
+        def MP(g):
+            state_passes(s_bank[g], [2 * g, 2 * g + 1])
+
+        def EP(g):
+            state_out(s_bank[g], g // 2, slice(64 * (g % 2), 64 * (g % 2) + 64))
+
+        def QP(g):
+            state_quant(g // 2, g, slice(0, 64 * (g % 2) + 64))
+            s_of[g] = g
+
+        def SU(s, u):
             nc.scalar.activation(
-                out=q_sq[2 * s + u][:].rearrange("p (c i) j -> p c j i", i=4),
-                in_=q_raw[2 * s + u].rearrange("p j (c i) -> p c j i", i=4),
+                out=q_sq[4 * s + u][:].rearrange("p r (m j) -> p m j r", j=4),
+                in_=q_raw[s][:, :, 128 * u : 128 * u + 128].rearrange("p j (m r) -> p m j r", r=4),
                 func=ACT.Square,
             )
 
-        def TQ(s, u, r):
+        def TU(s, u):
             nc.vector.scalar_tensor_tensor(
-                out=q_bf[2 * s + u][:, r],
-                in0=q_sq[2 * s + u][:].rearrange("p (m r) j -> p r m j", r=2)[:, r],
+                out=q_bf[s][:, :, 128 * u : 128 * u + 128],
+                in0=q_sq[4 * s + u][:],
                 scalar=0.125,
-                in1=qa_sb[:].unsqueeze(1).to_broadcast([P, 128, 4]),
+                in1=qa_rep[:].unsqueeze(1).to_broadcast([P, 4, 128]),
                 op0=ALU.add,
                 op1=ALU.mult,
             )
 
-        def QQ(s, u):
+        def QH(s, i):
             nc.vector.quantize_mx(
-                out=q_codes[2 * s + u][:].bitcast(FP8X4),
-                scales=q_scales[2 * s + u][:],
-                in_=q_bf[2 * s + u][:].rearrange("p r m j -> p (r m j)"),
+                out=q_codes[2 * s + i][:].bitcast(FP8X4),
+                scales=q_scales[2 * s + i][:],
+                in_=q_bf[s][:, 2 * i : 2 * i + 2, :].rearrange("p r m -> p (r m)"),
             )
 
-        def MY(s, u):
-            for r in range(2):
-                for c in range(4):
+        def MZ(g):
+            s = g // 2
+            for r in range(4):
+                for h in (2 * g, 2 * g + 1):
+                    c = h % 4
                     rows = slice(32 * c, 32 * c + 32)
-                    cols = slice(128 * r, 128 * r + 128)
-                    o = 256 * u + 128 * r
+                    cols = slice(128 * (r % 2), 128 * (r % 2) + 128)
                     nc.tensor.matmul_mx(
-                        out=y_bank[c][:, o : o + 128],
-                        lhsT=q_codes[2 * s + u][rows, cols].bitcast(FP8X4),
-                        lhsT_scale=q_scales[2 * s + u][rows, cols],
-                        rhs=s_codes[s][rows, :].bitcast(FP8X4),
-                        rhs_scale=s_scales[s][rows, :],
+                        out=y_bank[c][:, 128 * r : 128 * r + 128],
+                        lhsT=q_codes[2 * s + r // 2][rows, cols].bitcast(FP8X4),
+                        lhsT_scale=q_scales[2 * s + r // 2][rows, cols],
+                        rhs=s_codes[s_of[g]][rows, :].bitcast(FP8X4),
+                        rhs_scale=s_scales[s_of[g]][rows, :],
                         start=True,
                         stop=True,
                     )
 
-        def EA(s, u, c):
-            nc.scalar.copy(out=y_sb[4 * s + 2 * u + c // 2][:, c % 2, :], in_=y_bank[c][:, 256 * u : 256 * u + 256])
+        def MA(g):
+            MZ(g)
 
-        def EV(s, u, c):
-            nc.vector.tensor_copy(
-                out=y_sb[4 * s + 2 * u + c // 2][:, c % 2, :], in_=y_bank[c][:, 256 * u : 256 * u + 256]
-            )
+        def FA(h):
+            nc.scalar.copy(out=y_sb[h][:], in_=y_bank[h % 4][:])
 
-        def ST(s, u, g):
-            h0 = 4 * s + 2 * g
-            nc.sync.dma_start(
-                out=out[h0 : h0 + 2, 256 * u : 256 * u + 256, :].rearrange("c (p r) e -> p c (r e)", r=2),
-                in_=y_sb[4 * s + 2 * u + g][:],
-            )
+        def FV(h):
+            nc.vector.tensor_copy(out=y_sb[h][:], in_=y_bank[h % 4][:])
+
+        def SH(h):
+            nc.sync.dma_start(out=out[h].rearrange("(p r) e -> p (r e)", r=4), in_=y_sb[h][:])
 
         load_small()
         LK(0,1)
         LK(1,1)
         LK(2,2)
-        LQH(0,0)
-        LQH(0,1)
+        LK(4,2)
+        LQ(0)
         LV(0,2)
         LV(2,2)
-        LK(4,2)
         LK(6,2)
         LV(4,2)
+        LQ(1)
         LV(6,2)
-        LQH(1,0)
-        LQH(1,1)
         ZERO()
         W()
         SK(0)
         TK(0)
         SK(1)
         TK(1)
+        QA()
         SK(2)
         TK(2)
         QK(0)
         SK(3)
         TK(3)
         CK(0)
-        SQ(0,0)
-        QK(1)
-        TQ(0,0,0)
-        CK(1)
-        TQ(0,0,1)
-        SQ(0,1)
-        CVA(0)
-        CVA(1)
-        TQ(0,1,0)
-        QQ(0,0)
-        TQ(0,1,1)
-        QV(0)
-        QQ(0,1)
-        QV(1)
-        MS(0)
         SK(4)
-        SK(5)
         TK(4)
+        QK(1)
+        SK(5)
         TK(5)
-        SK(6)
-        ES(0)
-        SK(7)
+        CK(1)
         QK(2)
-        TK(6)
-        QS(0)
-        TK(7)
+        SU(0,0)
+        SU(0,1)
+        SU(0,2)
+        CHA(2)
+        SU(0,3)
+        TU(0,0)
+        CH(0)
+        CH(1)
+        TU(0,1)
+        CH(3)
+        QW(0)
+        QW(1)
+        MS(0)
         CK(2)
-        CV(2)
+        TU(0,2)
+        TU(0,3)
+        SK(6)
+        SK(7)
+        CHA(4)
+        CHA(5)
+        TK(6)
+        QH(0,0)
+        TK(7)
+        QW(2)
+        MP(2)
         QK(3)
-        QV(2)
+        QH(0,1)
+        ES(0)
+        QS(0)
+        MA(0)
+        MA(1)
         CK(3)
-        CV(3)
-        MY(0,0)
-        EA(0,0,0)
-        EA(0,0,1)
-        ST(0,0,0)
-        EA(0,0,2)
-        EA(0,0,3)
-        ST(0,0,1)
-        MY(0,1)
-        SQ(1,0)
-        QV(3)
-        MS(1)
-        TQ(1,0,0)
-        TQ(1,0,1)
-        EA(0,1,0)
-        EA(0,1,1)
-        ST(0,1,0)
-        SQ(1,1)
-        ES(1)
-        QQ(1,0)
-        TQ(1,1,0)
-        QS(1)
-        TQ(1,1,1)
-        EA(0,1,2)
-        EA(0,1,3)
-        ST(0,1,1)
-        MY(1,0)
-        QQ(1,1)
-        EA(1,0,0)
-        EA(1,0,1)
-        ST(1,0,0)
-        EV(1,0,2)
-        EV(1,0,3)
-        ST(1,0,1)
-        MY(1,1)
-        EA(1,1,0)
-        EA(1,1,1)
-        ST(1,1,0)
-        EV(1,1,2)
-        EV(1,1,3)
-        ST(1,1,1)
+        SU(1,0)
+        SU(1,1)
+        SU(1,2)
+        SU(1,3)
+        TU(1,0)
+        CH(6)
+        CH(7)
+        TU(1,1)
+        QW(3)
+        MP(3)
+        EP(2)
+        FA(0)
+        SH(0)
+        FA(1)
+        SH(1)
+        FA(2)
+        SH(2)
+        EP(3)
+        TU(1,2)
+        TU(1,3)
+        QP(2)
+        QH(1,0)
+        QH(1,1)
+        MZ(2)
+        FV(3)
+        SH(3)
+        QP(3)
+        MZ(3)
+        FA(4)
+        SH(4)
+        FV(5)
+        SH(5)
+        FA(6)
+        FV(7)
+        SH(6)
+        SH(7)

@@ -3,7 +3,7 @@ from contextlib import ExitStack
 import concourse.mybir as mybir
 
 H, D, N = 8, 128, 512
-FLOPS = 2 * 2 * H * N * D * 128
+FLOPS = 2 * 2 * H * N * D * D
 
 F32 = mybir.dt.float32
 BF16 = mybir.dt.bfloat16
@@ -15,6 +15,13 @@ ACT = mybir.ActivationFunctionType
 ALU = mybir.AluOpType
 
 P = 128
+PACK = 4
+ROWS = D // PACK
+COLS = 128
+BANK = PACK * COLS
+PAIRS, SETS = H // 2, H // 4
+PHI_OFFSET = 0.125
+MARGIN = 2 * ROWS
 
 
 def tile_rows_lin_sq_kernel(tc, q, qa, ka, k, t, v, out):
@@ -28,348 +35,274 @@ def tile_rows_lin_sq_kernel(tc, q, qa, ka, k, t, v, out):
             return [sb.tile(shape, dtype, name="%s%d" % (name, i), align_bytes=64) for i in range(count)]
 
         ka_sb = sb.tile([P, D], F32, name="ka_sb")
-        t_sb = sb.tile([P, 4], F32, name="t_sb")
-        qa_sb = sb.tile([P, 4], F32, name="qa_sb")
-        qa_rep = sb.tile([P, 128], F32, name="qa_rep")
-        w = sb.tile([P, 512], F32, name="w")
-        k_raw = {}
-        v_raw = {}
-        q_raw = {}
-        k_sq = tiles("k_sq", 8, [P, 512], F32)
-        k_bf = tiles("k_bf", 4, [P, 4, 2, 128], BF16)
-        k_codes = tiles("k_codes", 4, [P, 256], U32)
-        k_scales = tiles("k_scales", 4, [P, 384], U8)
-        k_pad = tiles("k_pad", 4, [P, 1152], U32)
-        v_bf = tiles("v_bf", 4, [P, 2, 128, 4], BF16)
-        v_codes = tiles("v_codes", 4, [P, 256], U32)
-        v_scales = tiles("v_scales", 4, [P, 256], U8)
-        q_sq = tiles("q_sq", 8, [P, 4, 128], F32)
-        q_bf = tiles("q_bf", 2, [P, 4, 512], BF16)
-        q_codes = tiles("q_codes", 4, [P, 256], U32)
-        q_scales = tiles("q_scales", 4, [P, 256], U8)
-        s_bf = tiles("s_bf", 2, [P, 128, 4], BF16)
-        s_codes = tiles("s_codes", 4, [P, 128], U32)
-        s_scales = tiles("s_scales", 4, [P, 128], U8)
-        y_sb = tiles("y_sb", 8, [P, 512], F32)
-        s_bank = [ps.tile([P, 512], F32, name="s_bank%d" % i) for i in range(4)]
-        s_of = {}
-        y_bank = [ps.tile([P, 512], F32, name="y_bank%d" % i) for i in range(4)]
+        t_sb = sb.tile([P, PACK], F32, name="t_sb")
+        qa_sb = sb.tile([P, PACK], F32, name="qa_sb")
+        qa_rep = sb.tile([P, ROWS * PACK], F32, name="qa_rep")
+        k_weight = sb.tile([P, BANK], F32, name="k_weight")
+        k_raw, v_raw, q_raw = {}, {}, {}
+        k_sq = tiles("k_sq", H, [P, BANK], F32)
+        k_bf = tiles("k_bf", PAIRS, [P, PACK, 2, COLS], BF16)
+        k_codes = tiles("k_codes", PAIRS, [P, 2 * COLS], U32)
+        k_scales = tiles("k_scales", PAIRS, [P, 2 * COLS + 2 * MARGIN], U8)
+        k_spread = tiles("k_spread", PAIRS, [P, 2 * BANK + COLS], U32)
+        v_bf = tiles("v_bf", PAIRS, [P, 2, COLS, PACK], BF16)
+        v_codes = tiles("v_codes", PAIRS, [P, 2 * COLS], U32)
+        v_scales = tiles("v_scales", PAIRS, [P, 2 * COLS], U8)
+        q_sq = tiles("q_sq", SETS * PACK, [P, PACK, COLS], F32)
+        q_bf = tiles("q_bf", SETS, [P, PACK, BANK], BF16)
+        q_codes = tiles("q_codes", SETS * 2, [P, 2 * COLS], U32)
+        q_scales = tiles("q_scales", SETS * 2, [P, 2 * COLS], U8)
+        s_bf = tiles("s_bf", SETS, [P, COLS, PACK], BF16)
+        y_sb = tiles("y_sb", H, [P, BANK], F32)
 
-        def load_small():
-            nc.scalar.dma_start(out=ka_sb[:], in_=ka)
-            nc.scalar.dma_start(out=t_sb[:], in_=t.rearrange("(p j) o -> p (j o)", j=4))
-            nc.scalar.dma_start(
-                out=qa_sb[:],
-                in_=qa.rearrange("(o p j) z -> o p (j z)", o=1, j=4).to_broadcast([4, 32, 4]),
-            )
+        state_parts = [range(0, 4), range(4, 6), range(6, 8)]
+        s_codes = tiles("s_codes", len(state_parts), [P, COLS], U32)
+        s_scales = tiles("s_scales", len(state_parts), [P, COLS], U8)
+        s_bank = [ps.tile([P, BANK], F32, name="s_bank%d" % i) for i in range(len(state_parts))]
+        y_bank = [ps.tile([P, BANK], F32, name="y_bank%d" % c) for c in range(PACK)]
 
-        def load_rows(src, store, name, h0, count):
-            raw = sb.tile([P, count, 4, 128], F32, name="%s%d" % (name, h0))
+        def load_tokens(src, raws, name, first, count):
+            raw = sb.tile([P, count, PACK, D], F32, name="%s%d" % (name, first))
             nc.sync.dma_start(
                 out=raw[:].rearrange("p h j d -> p h (j d)"),
-                in_=src[h0 : h0 + count].rearrange("h (p j) d -> p h (j d)", j=4),
+                in_=src[first : first + count].rearrange("h (p j) d -> p h (j d)", j=PACK),
             )
             for i in range(count):
-                store[h0 + i] = (raw, i)
+                raws[first + i] = raw[:, i]
 
-        def LK(h0, count):
-            load_rows(k, k_raw, "k_raw", h0, count)
+        def load_keys(first, count):
+            load_tokens(k, k_raw, "k_raw", first, count)
 
-        def LV(h0, count):
-            load_rows(v, v_raw, "v_raw", h0, count)
+        def load_values(g):
+            load_tokens(v, v_raw, "v_raw", 2 * g, 2)
 
-        def LQ(s):
-            raw = sb.tile([P, 4, 512], F32, name="q_raw%d" % s)
-            nc.sync.dma_start(out=raw[:], in_=q[4 * s : 4 * s + 4].rearrange("c (p j) n -> (c p) j n", j=4))
-            q_raw[s] = raw
-
-        def LQH(s, u):
-            raw = sb.tile([P, 4, 256], F32, name="q_rawh%d" % (2 * s + u))
+        def load_queries(s):
+            q_raw[s] = sb.tile([P, PACK, N], F32, name="q_raw%d" % s)
             nc.sync.dma_start(
-                out=raw[:],
-                in_=q[4 * s : 4 * s + 4].rearrange("c (p j) n -> (c p) j n", j=4)[:, :, 256 * u : 256 * u + 256],
-            )
-            q_raw[2 * s + u] = raw[:]
-
-        def ZERO():
-            for g in range(4):
-                nc.gpsimd.memset(k_pad[g][:], 0)
-            for g in range(4):
-                nc.gpsimd.memset(k_scales[g][:].bitcast(U32), 0)
-
-        def W():
-            nc.vector.tensor_tensor(
-                out=w[:].rearrange("p (x m j) -> p x m j", x=4, j=4),
-                in0=ka_sb[:].rearrange("p (m x) -> p x m", x=4).unsqueeze(3).to_broadcast([P, 4, 32, 4]),
-                in1=t_sb[:].unsqueeze(1).unsqueeze(1).to_broadcast([P, 4, 32, 4]),
-                op=ALU.mult,
+                out=q_raw[s][:], in_=q[4 * s : 4 * s + 4].rearrange("c (m j) n -> (c m) j n", j=PACK)
             )
 
-
-        def QA():
-            nc.vector.tensor_copy(
-                out=qa_rep[:].rearrange("p (m j) -> p m j", j=4),
-                in_=qa_sb[:].unsqueeze(1).to_broadcast([P, 32, 4]),
-            )
-
-        def SK(h):
-            raw, i = k_raw[h]
+        def square_keys(h):
             nc.scalar.activation(
-                out=k_sq[h][:].rearrange("p (x m j) -> p m j x", x=4, j=4),
-                in_=raw[:, i].rearrange("p j (m x) -> p m j x", x=4),
+                out=k_sq[h][:].rearrange("p (x m j) -> p m j x", x=PACK, j=PACK),
+                in_=k_raw[h].rearrange("p j (m x) -> p m j x", x=PACK),
                 func=ACT.Square,
             )
 
-        def TK(h):
+        def weigh_keys(h):
             nc.vector.scalar_tensor_tensor(
                 out=k_bf[h // 2][:, :, h % 2, :],
-                in0=k_sq[h][:].rearrange("p (x r) -> p x r", x=4),
-                scalar=0.125,
-                in1=w[:].rearrange("p (x r) -> p x r", x=4),
+                in0=k_sq[h][:].rearrange("p (x r) -> p x r", x=PACK),
+                scalar=PHI_OFFSET,
+                in1=k_weight[:].rearrange("p (x r) -> p x r", x=PACK),
                 op0=ALU.add,
                 op1=ALU.mult,
             )
 
-        def QK(g):
+        def quantise_keys(g):
             nc.vector.quantize_mx(
                 out=k_codes[g][:].bitcast(FP8X4),
-                scales=k_scales[g][:, 64:320],
+                scales=k_scales[g][:, MARGIN : MARGIN + 2 * COLS],
                 in_=k_bf[g][:].rearrange("p x c r -> p (x c r)"),
             )
 
-        def CK(g):
-            base = 64 * (g % 2)
-            dst = k_pad[g][:, base : base + 1088].bitcast(I32).rearrange("p (c r) -> p c r", c=2)
-            dst = dst[:, :, 0:512].rearrange("p c (x m) -> p c x m", x=4)[:, :, :, 0:32]
+        def spread_keys(g):
+            first = 2 * ROWS * (g % 2)
+            step = BANK + ROWS
+            dst = k_spread[g][:, first : first + 2 * step].bitcast(I32).rearrange("p (c r) -> p c r", c=2)
+            dst = dst[:, :, 0:BANK].rearrange("p c (x m) -> p c x m", x=PACK)[:, :, :, 0:ROWS]
             nc.vector.tensor_copy(
-                out=dst, in_=k_codes[g][:].bitcast(I32).rearrange("p (x c m) -> p c x m", x=4, c=2)
+                out=dst, in_=k_codes[g][:].bitcast(I32).rearrange("p (x c m) -> p c x m", x=PACK, c=2)
             )
 
-        def ch_views(h):
-            raw, i = v_raw[h]
-            return (
-                v_bf[h // 2][:, h % 2].rearrange("p (c i) j -> p c j i", i=4),
-                raw[:, i].rearrange("p j (c i) -> p c j i", i=4),
+        def cast_values(h, copy):
+            copy(
+                out=v_bf[h // 2][:, h % 2].rearrange("p (b i) j -> p b j i", i=PACK),
+                in_=v_raw[h].rearrange("p j (b i) -> p b j i", i=PACK),
             )
 
-        def CH(h):
-            dst, src = ch_views(h)
-            nc.vector.tensor_copy(out=dst, in_=src)
-
-        def CHA(h):
-            dst, src = ch_views(h)
-            nc.scalar.copy(out=dst, in_=src)
-
-        def QW(g):
+        def quantise_values(g):
             nc.vector.quantize_mx(
                 out=v_codes[g][:].bitcast(FP8X4),
                 scales=v_scales[g][:],
                 in_=v_bf[g][:].rearrange("p h e j -> p (h e j)"),
             )
 
-        def state_passes(bank, heads):
-            for x in range(4):
+        def multiply_state(part):
+            heads = state_parts[part]
+            for x in range(PACK):
                 for h in heads:
-                    g, c = h // 2, h % 4
-                    col = 512 * (h % 2) + 128 * x
-                    sc = 64 + 64 * x - 64 * (c // 2)
-                    e0 = 128 * (h % 2)
+                    g = h // 2
+                    operand = BANK * (h % 2) + COLS * x
+                    window = MARGIN + 2 * ROWS * (x - g % 2)
+                    e_cols = slice(COLS * (h % 2), COLS * (h % 2) + COLS)
                     nc.tensor.matmul_mx(
-                        out=bank[:, 128 * x : 128 * x + 128],
-                        lhsT=k_pad[g][:, col : col + 128].bitcast(FP8X4),
-                        lhsT_scale=k_scales[g][:, sc : sc + 128],
-                        rhs=v_codes[g][:, e0 : e0 + 128].bitcast(FP8X4),
-                        rhs_scale=v_scales[g][:, e0 : e0 + 128],
+                        out=s_bank[part][:, COLS * x : COLS * x + COLS],
+                        lhsT=k_spread[g][:, operand : operand + COLS].bitcast(FP8X4),
+                        lhsT_scale=k_scales[g][:, window : window + COLS],
+                        rhs=v_codes[g][:, e_cols].bitcast(FP8X4),
+                        rhs_scale=v_scales[g][:, e_cols],
                         start=(h == heads[0]),
                         stop=(h == heads[-1]),
                     )
 
-        def state_out(bank, s, rows):
+        def round_state(part):
+            heads = state_parts[part]
+            rows = slice(ROWS * (heads[0] % 4), ROWS * (heads[-1] % 4 + 1))
             nc.scalar.activation(
-                out=s_bf[s][rows],
-                in_=bank[rows, :].rearrange("p (x e) -> p e x", x=4),
+                out=s_bf[heads[0] // 4][rows],
+                in_=s_bank[part][rows, :].rearrange("p (x e) -> p e x", x=PACK),
                 func=ACT.Copy,
                 scale=1.0 / N,
             )
 
-        def state_quant(s, i, rows):
+        def quantise_state(part):
+            heads = state_parts[part]
+            rows = slice(0, ROWS * (heads[-1] % 4 + 1))
             nc.vector.quantize_mx(
-                out=s_codes[i][rows, :].bitcast(FP8X4),
-                scales=s_scales[i][rows, :],
-                in_=s_bf[s][rows].rearrange("p e x -> p (e x)"),
+                out=s_codes[part][rows, :].bitcast(FP8X4),
+                scales=s_scales[part][rows, :],
+                in_=s_bf[heads[0] // 4][rows].rearrange("p e x -> p (e x)"),
             )
 
-        def MS(s):
-            state_passes(s_bank[2 * s], [4 * s, 4 * s + 1, 4 * s + 2, 4 * s + 3])
-
-        def ES(s):
-            state_out(s_bank[2 * s], s, slice(0, 128))
-
-        def QS(s):
-            state_quant(s, 2 * s, slice(0, 128))
-            s_of[2 * s] = 2 * s
-            s_of[2 * s + 1] = 2 * s
-
-        def MP(g):
-            state_passes(s_bank[g], [2 * g, 2 * g + 1])
-
-        def EP(g):
-            state_out(s_bank[g], g // 2, slice(64 * (g % 2), 64 * (g % 2) + 64))
-
-        def QP(g):
-            state_quant(g // 2, g, slice(0, 64 * (g % 2) + 64))
-            s_of[g] = g
-
-        def SU(s, u):
+        def square_queries(s, u):
             nc.scalar.activation(
-                out=q_sq[4 * s + u][:].rearrange("p r (m j) -> p m j r", j=4),
-                in_=q_raw[s][:, :, 128 * u : 128 * u + 128].rearrange("p j (m r) -> p m j r", r=4),
+                out=q_sq[PACK * s + u][:].rearrange("p r (m j) -> p m j r", j=PACK),
+                in_=q_raw[s][:, :, COLS * u : COLS * u + COLS].rearrange("p j (m r) -> p m j r", r=PACK),
                 func=ACT.Square,
             )
 
-        def TU(s, u):
+        def weigh_queries(s, u):
             nc.vector.scalar_tensor_tensor(
-                out=q_bf[s][:, :, 128 * u : 128 * u + 128],
-                in0=q_sq[4 * s + u][:],
-                scalar=0.125,
-                in1=qa_rep[:].unsqueeze(1).to_broadcast([P, 4, 128]),
+                out=q_bf[s][:, :, COLS * u : COLS * u + COLS],
+                in0=q_sq[PACK * s + u][:],
+                scalar=PHI_OFFSET,
+                in1=qa_rep[:].unsqueeze(1).to_broadcast([P, PACK, COLS]),
                 op0=ALU.add,
                 op1=ALU.mult,
             )
 
-        def QH(s, i):
+        def quantise_queries(s, half):
             nc.vector.quantize_mx(
-                out=q_codes[2 * s + i][:].bitcast(FP8X4),
-                scales=q_scales[2 * s + i][:],
-                in_=q_bf[s][:, 2 * i : 2 * i + 2, :].rearrange("p r m -> p (r m)"),
+                out=q_codes[2 * s + half][:].bitcast(FP8X4),
+                scales=q_scales[2 * s + half][:],
+                in_=q_bf[s][:, 2 * half : 2 * half + 2, :].rearrange("p r m -> p (r m)"),
             )
 
-        def MZ(g):
-            s = g // 2
-            for r in range(4):
+        def multiply_result(g, part):
+            for r in range(PACK):
                 for h in (2 * g, 2 * g + 1):
-                    c = h % 4
-                    rows = slice(32 * c, 32 * c + 32)
-                    cols = slice(128 * (r % 2), 128 * (r % 2) + 128)
+                    rows = slice(ROWS * (h % 4), ROWS * (h % 4) + ROWS)
+                    cols = slice(COLS * (r % 2), COLS * (r % 2) + COLS)
+                    half = 2 * (h // 4) + r // 2
                     nc.tensor.matmul_mx(
-                        out=y_bank[c][:, 128 * r : 128 * r + 128],
-                        lhsT=q_codes[2 * s + r // 2][rows, cols].bitcast(FP8X4),
-                        lhsT_scale=q_scales[2 * s + r // 2][rows, cols],
-                        rhs=s_codes[s_of[g]][rows, :].bitcast(FP8X4),
-                        rhs_scale=s_scales[s_of[g]][rows, :],
+                        out=y_bank[h % 4][:, COLS * r : COLS * r + COLS],
+                        lhsT=q_codes[half][rows, cols].bitcast(FP8X4),
+                        lhsT_scale=q_scales[half][rows, cols],
+                        rhs=s_codes[part][rows, :].bitcast(FP8X4),
+                        rhs_scale=s_scales[part][rows, :],
                         start=True,
                         stop=True,
                     )
 
-        def MA(g):
-            MZ(g)
+        def store_result(h, copy):
+            copy(out=y_sb[h][:], in_=y_bank[h % 4][:])
+            nc.sync.dma_start(out=out[h].rearrange("(m r) e -> m (r e)", r=PACK), in_=y_sb[h][:])
 
-        def FA(h):
-            nc.scalar.copy(out=y_sb[h][:], in_=y_bank[h % 4][:])
+        on_scalar, on_vector = nc.scalar.copy, nc.vector.tensor_copy
 
-        def FV(h):
-            nc.vector.tensor_copy(out=y_sb[h][:], in_=y_bank[h % 4][:])
+        nc.scalar.dma_start(out=ka_sb[:], in_=ka)
+        nc.scalar.dma_start(out=t_sb[:], in_=t.rearrange("(p j) o -> p (j o)", j=PACK))
+        nc.scalar.dma_start(
+            out=qa_sb[:],
+            in_=qa.rearrange("(o m j) z -> o m (j z)", o=1, j=PACK).to_broadcast([PACK, ROWS, PACK]),
+        )
 
-        def SH(h):
-            nc.sync.dma_start(out=out[h].rearrange("(p r) e -> p (r e)", r=4), in_=y_sb[h][:])
+        for h in range(4):
+            load_keys(h, 1)
+        load_keys(4, 2)
+        load_queries(0)
+        load_values(0)
+        load_values(1)
+        load_keys(6, 2)
+        load_values(2)
+        load_queries(1)
+        load_values(3)
 
-        load_small()
-        LK(0,1)
-        LK(1,1)
-        LK(2,2)
-        LK(4,2)
-        LQ(0)
-        LV(0,2)
-        LV(2,2)
-        LK(6,2)
-        LV(4,2)
-        LQ(1)
-        LV(6,2)
-        ZERO()
-        W()
-        SK(0)
-        TK(0)
-        SK(1)
-        TK(1)
-        QA()
-        SK(2)
-        TK(2)
-        QK(0)
-        SK(3)
-        TK(3)
-        CK(0)
-        SK(4)
-        TK(4)
-        QK(1)
-        SK(5)
-        TK(5)
-        CK(1)
-        QK(2)
-        SU(0,0)
-        SU(0,1)
-        SU(0,2)
-        CHA(2)
-        SU(0,3)
-        TU(0,0)
-        CH(0)
-        CH(1)
-        TU(0,1)
-        CH(3)
-        QW(0)
-        QW(1)
-        MS(0)
-        CK(2)
-        TU(0,2)
-        TU(0,3)
-        SK(6)
-        SK(7)
-        CHA(4)
-        CHA(5)
-        TK(6)
-        QH(0,0)
-        TK(7)
-        QW(2)
-        MP(2)
-        QK(3)
-        QH(0,1)
-        ES(0)
-        QS(0)
-        MA(0)
-        MA(1)
-        CK(3)
-        SU(1,0)
-        SU(1,1)
-        SU(1,2)
-        SU(1,3)
-        TU(1,0)
-        CH(6)
-        CH(7)
-        TU(1,1)
-        QW(3)
-        MP(3)
-        EP(2)
-        FA(0)
-        SH(0)
-        FA(1)
-        SH(1)
-        FA(2)
-        SH(2)
-        EP(3)
-        TU(1,2)
-        TU(1,3)
-        QP(2)
-        QH(1,0)
-        QH(1,1)
-        MZ(2)
-        FV(3)
-        SH(3)
-        QP(3)
-        MZ(3)
-        FA(4)
-        SH(4)
-        FV(5)
-        SH(5)
-        FA(6)
-        FV(7)
-        SH(6)
-        SH(7)
+        for g in range(PAIRS):
+            nc.gpsimd.memset(k_spread[g][:, 0 : 2 * BANK], 0)
+        for g in range(PAIRS):
+            nc.gpsimd.memset(k_scales[g][:].bitcast(U32), 0)
+
+        nc.vector.tensor_tensor(
+            out=k_weight[:].rearrange("p (x m j) -> p x m j", x=PACK, j=PACK),
+            in0=ka_sb[:].rearrange("p (m x) -> p x m", x=PACK).unsqueeze(3).to_broadcast([P, PACK, ROWS, PACK]),
+            in1=t_sb[:].unsqueeze(1).unsqueeze(1).to_broadcast([P, PACK, ROWS, PACK]),
+            op=ALU.mult,
+        )
+
+        for h in range(6):
+            square_keys(h)
+            weigh_keys(h)
+            if h >= 2 and h % 2 == 0:
+                quantise_keys(h // 2 - 1)
+            if h >= 2 and h % 2 == 1:
+                spread_keys(h // 2 - 1)
+        quantise_keys(2)
+        nc.vector.tensor_copy(
+            out=qa_rep[:].rearrange("p (m j) -> p m j", j=PACK),
+            in_=qa_sb[:].unsqueeze(1).to_broadcast([P, ROWS, PACK]),
+        )
+
+        square_queries(0, 0)
+        square_queries(0, 1)
+        weigh_queries(0, 0)
+        for g in range(2):
+            cast_values(2 * g, on_scalar)
+            square_queries(0, g + 2)
+            cast_values(2 * g + 1, on_vector)
+            weigh_queries(0, g + 1)
+            quantise_values(g)
+        multiply_state(0)
+        weigh_queries(0, 3)
+        spread_keys(2)
+
+        for i in range(2):
+            square_keys(6 + i)
+            weigh_keys(6 + i)
+            quantise_queries(0, i)
+        for h in state_parts[1]:
+            cast_values(h, on_scalar)
+        quantise_values(2)
+        multiply_state(1)
+        quantise_keys(3)
+        round_state(0)
+        quantise_state(0)
+        for g in range(2):
+            multiply_result(g, 0)
+        spread_keys(3)
+
+        for u in range(PACK):
+            square_queries(1, u)
+        weigh_queries(1, 0)
+        for h in state_parts[2]:
+            cast_values(h, on_vector)
+        weigh_queries(1, 1)
+        quantise_values(3)
+        multiply_state(2)
+
+        round_state(1)
+        for h in range(3):
+            store_result(h, on_scalar)
+        round_state(2)
+        weigh_queries(1, 2)
+        weigh_queries(1, 3)
+        quantise_state(1)
+        quantise_queries(1, 0)
+        quantise_queries(1, 1)
+        multiply_result(2, 1)
+        store_result(3, on_vector)
+        quantise_state(2)
+        multiply_result(3, 2)
+        for h in range(4, H):
+            store_result(h, on_vector if h % 2 else on_scalar)

@@ -213,15 +213,15 @@ def tile_rows_lin_sq_kernel(tc, q, qa, ka, k, t, v, out):
 
         nc.scalar.dma_start(out=ka_sb[:], in_=ka)
         nc.scalar.dma_start(out=t_sb[:], in_=t.rearrange("(p j) o -> p (j o)", j=PACK))
-        nc.scalar.dma_start(
-            out=qa_sb[:],
-            in_=qa.rearrange("(o m j) z -> o m (j z)", o=1, j=PACK).to_broadcast([PACK, ROWS, PACK]),
-        )
 
         for h in range(4):
             load_keys(h, 1)
         load_keys(4, 2)
         load_queries(0)
+        nc.sync.dma_start(
+            out=qa_sb[:],
+            in_=qa.rearrange("(o m j) z -> o m (j z)", o=1, j=PACK).to_broadcast([PACK, ROWS, PACK]),
+        )
         load_values(0)
         load_values(1)
         load_keys(6, 2)
@@ -230,9 +230,8 @@ def tile_rows_lin_sq_kernel(tc, q, qa, ka, k, t, v, out):
         load_values(3)
 
         for g in range(PAIRS):
-            nc.gpsimd.memset(k_spread[g][:, 0 : 2 * BANK], 0)
-        for g in range(PAIRS):
             nc.gpsimd.memset(k_scales[g][:].bitcast(U32), 0)
+            nc.gpsimd.memset(k_spread[g][:, 0 : 2 * BANK], 0)
 
         nc.vector.tensor_tensor(
             out=k_weight[:].rearrange("p (x m j) -> p x m j", x=PACK, j=PACK),
@@ -248,11 +247,11 @@ def tile_rows_lin_sq_kernel(tc, q, qa, ka, k, t, v, out):
                 quantise_keys(h // 2 - 1)
             if h >= 2 and h % 2 == 1:
                 spread_keys(h // 2 - 1)
-        quantise_keys(2)
         nc.vector.tensor_copy(
             out=qa_rep[:].rearrange("p (m j) -> p m j", j=PACK),
             in_=qa_sb[:].unsqueeze(1).to_broadcast([P, ROWS, PACK]),
         )
+        quantise_keys(2)
 
         square_queries(0, 0)
         square_queries(0, 1)

from contextlib import ExitStack

import concourse.mybir as mybir

H, D, N = 8, 128, 512
FLOPS = 2 * 2 * H * N * D * D

F32 = mybir.dt.float32
BF16 = mybir.dt.bfloat16
U32 = mybir.dt.uint32
I32 = mybir.dt.int32
U8 = mybir.dt.uint8
FP8X4 = mybir.dt.float8_e4m3fn_x4
ACT = mybir.ActivationFunctionType
ALU = mybir.AluOpType

P = 128
PACK = 4
ROWS = D // PACK
COLS = 128
BANK = PACK * COLS
PAIRS, SETS = H // 2, H // 4
PHI_OFFSET = 0.125
MARGIN = 2 * ROWS


def tile_rows_lin_sq_kernel(tc, q, qa, ka, k, t, v, out):
    nc = tc.nc
    with ExitStack() as ctx:
        sb = ctx.enter_context(tc.tile_pool(name="sb", bufs=1))
        ps = ctx.enter_context(tc.psum_pool(name="ps", bufs=1))
        ctx.enter_context(tc.manual_schedule())

        def tiles(name, count, shape, dtype):
            return [sb.tile(shape, dtype, name="%s%d" % (name, i), align_bytes=64) for i in range(count)]

        ka_sb = sb.tile([P, D], F32, name="ka_sb")
        t_sb = sb.tile([P, PACK], F32, name="t_sb")
        qa_sb = sb.tile([P, PACK], F32, name="qa_sb")
        qa_rep = sb.tile([P, ROWS * PACK], F32, name="qa_rep")
        k_weight = sb.tile([P, BANK], F32, name="k_weight")
        k_raw, v_raw, q_raw = {}, {}, {}
        k_sq = tiles("k_sq", H, [P, BANK], F32)
        k_bf = tiles("k_bf", PAIRS, [P, PACK, 2, COLS], BF16)
        k_codes = tiles("k_codes", PAIRS, [P, 2 * COLS], U32)
        k_scales = tiles("k_scales", PAIRS, [P, 2 * COLS + 2 * MARGIN], U8)
        k_spread = tiles("k_spread", PAIRS, [P, 2 * BANK + COLS], U32)
        v_bf = tiles("v_bf", PAIRS, [P, 2, COLS, PACK], BF16)
        v_codes = tiles("v_codes", PAIRS, [P, 2 * COLS], U32)
        v_scales = tiles("v_scales", PAIRS, [P, 2 * COLS], U8)
        q_sq = tiles("q_sq", SETS * PACK, [P, PACK, COLS], F32)
        q_bf = tiles("q_bf", SETS, [P, PACK, BANK], BF16)
        q_codes = tiles("q_codes", SETS * 2, [P, 2 * COLS], U32)
        q_scales = tiles("q_scales", SETS * 2, [P, 2 * COLS], U8)
        s_bf = tiles("s_bf", SETS, [P, COLS, PACK], BF16)
        y_sb = tiles("y_sb", H, [P, BANK], F32)

        state_parts = [range(0, 4), range(4, 6), range(6, 8)]
        s_codes = tiles("s_codes", len(state_parts), [P, COLS], U32)
        s_scales = tiles("s_scales", len(state_parts), [P, COLS], U8)
        s_bank = [ps.tile([P, BANK], F32, name="s_bank%d" % i) for i in range(len(state_parts))]
        y_bank = [ps.tile([P, BANK], F32, name="y_bank%d" % c) for c in range(PACK)]

        def load_tokens(src, raws, name, first, count):
            raw = sb.tile([P, count, PACK, D], F32, name="%s%d" % (name, first))
            nc.sync.dma_start(
                out=raw[:].rearrange("p h j d -> p h (j d)"),
                in_=src[first : first + count].rearrange("h (p j) d -> p h (j d)", j=PACK),
            )
            for i in range(count):
                raws[first + i] = raw[:, i]

        def load_keys(first, count):
            load_tokens(k, k_raw, "k_raw", first, count)

        def load_values(g):
            load_tokens(v, v_raw, "v_raw", 2 * g, 2)

        def load_queries(s):
            q_raw[s] = sb.tile([P, PACK, N], F32, name="q_raw%d" % s)
            nc.sync.dma_start(
                out=q_raw[s][:], in_=q[4 * s : 4 * s + 4].rearrange("c (m j) n -> (c m) j n", j=PACK)
            )

        def square_keys(h):
            nc.scalar.activation(
                out=k_sq[h][:].rearrange("p (x m j) -> p m j x", x=PACK, j=PACK),
                in_=k_raw[h].rearrange("p j (m x) -> p m j x", x=PACK),
                func=ACT.Square,
            )

        def weigh_keys(h):
            nc.vector.scalar_tensor_tensor(
                out=k_bf[h // 2][:, :, h % 2, :],
                in0=k_sq[h][:].rearrange("p (x r) -> p x r", x=PACK),
                scalar=PHI_OFFSET,
                in1=k_weight[:].rearrange("p (x r) -> p x r", x=PACK),
                op0=ALU.add,
                op1=ALU.mult,
            )

        def quantise_keys(g):
            nc.vector.quantize_mx(
                out=k_codes[g][:].bitcast(FP8X4),
                scales=k_scales[g][:, MARGIN : MARGIN + 2 * COLS],
                in_=k_bf[g][:].rearrange("p x c r -> p (x c r)"),
            )

        def spread_keys(g):
            first = 2 * ROWS * (g % 2)
            step = BANK + ROWS
            dst = k_spread[g][:, first : first + 2 * step].bitcast(I32).rearrange("p (c r) -> p c r", c=2)
            dst = dst[:, :, 0:BANK].rearrange("p c (x m) -> p c x m", x=PACK)[:, :, :, 0:ROWS]
            nc.vector.tensor_copy(
                out=dst, in_=k_codes[g][:].bitcast(I32).rearrange("p (x c m) -> p c x m", x=PACK, c=2)
            )

        def cast_values(h, copy):
            copy(
                out=v_bf[h // 2][:, h % 2].rearrange("p (b i) j -> p b j i", i=PACK),
                in_=v_raw[h].rearrange("p j (b i) -> p b j i", i=PACK),
            )

        def quantise_values(g):
            nc.vector.quantize_mx(
                out=v_codes[g][:].bitcast(FP8X4),
                scales=v_scales[g][:],
                in_=v_bf[g][:].rearrange("p h e j -> p (h e j)"),
            )

        def multiply_state(part):
            heads = state_parts[part]
            for x in range(PACK):
                for h in heads:
                    g = h // 2
                    operand = BANK * (h % 2) + COLS * x
                    window = MARGIN + 2 * ROWS * (x - g % 2)
                    e_cols = slice(COLS * (h % 2), COLS * (h % 2) + COLS)
                    nc.tensor.matmul_mx(
                        out=s_bank[part][:, COLS * x : COLS * x + COLS],
                        lhsT=k_spread[g][:, operand : operand + COLS].bitcast(FP8X4),
                        lhsT_scale=k_scales[g][:, window : window + COLS],
                        rhs=v_codes[g][:, e_cols].bitcast(FP8X4),
                        rhs_scale=v_scales[g][:, e_cols],
                        start=(h == heads[0]),
                        stop=(h == heads[-1]),
                    )

        def round_state(part):
            heads = state_parts[part]
            rows = slice(ROWS * (heads[0] % 4), ROWS * (heads[-1] % 4 + 1))
            nc.scalar.activation(
                out=s_bf[heads[0] // 4][rows],
                in_=s_bank[part][rows, :].rearrange("p (x e) -> p e x", x=PACK),
                func=ACT.Copy,
                scale=1.0 / N,
            )

        def quantise_state(part):
            heads = state_parts[part]
            rows = slice(0, ROWS * (heads[-1] % 4 + 1))
            nc.vector.quantize_mx(
                out=s_codes[part][rows, :].bitcast(FP8X4),
                scales=s_scales[part][rows, :],
                in_=s_bf[heads[0] // 4][rows].rearrange("p e x -> p (e x)"),
            )

        def square_queries(s, u):
            nc.scalar.activation(
                out=q_sq[PACK * s + u][:].rearrange("p r (m j) -> p m j r", j=PACK),
                in_=q_raw[s][:, :, COLS * u : COLS * u + COLS].rearrange("p j (m r) -> p m j r", r=PACK),
                func=ACT.Square,
            )

        def weigh_queries(s, u):
            nc.vector.scalar_tensor_tensor(
                out=q_bf[s][:, :, COLS * u : COLS * u + COLS],
                in0=q_sq[PACK * s + u][:],
                scalar=PHI_OFFSET,
                in1=qa_rep[:].unsqueeze(1).to_broadcast([P, PACK, COLS]),
                op0=ALU.add,
                op1=ALU.mult,
            )

        def quantise_queries(s, half):
            nc.vector.quantize_mx(
                out=q_codes[2 * s + half][:].bitcast(FP8X4),
                scales=q_scales[2 * s + half][:],
                in_=q_bf[s][:, 2 * half : 2 * half + 2, :].rearrange("p r m -> p (r m)"),
            )

        def multiply_result(g, part):
            for r in range(PACK):
                for h in (2 * g, 2 * g + 1):
                    rows = slice(ROWS * (h % 4), ROWS * (h % 4) + ROWS)
                    cols = slice(COLS * (r % 2), COLS * (r % 2) + COLS)
                    half = 2 * (h // 4) + r // 2
                    nc.tensor.matmul_mx(
                        out=y_bank[h % 4][:, COLS * r : COLS * r + COLS],
                        lhsT=q_codes[half][rows, cols].bitcast(FP8X4),
                        lhsT_scale=q_scales[half][rows, cols],
                        rhs=s_codes[part][rows, :].bitcast(FP8X4),
                        rhs_scale=s_scales[part][rows, :],
                        start=True,
                        stop=True,
                    )

        def store_result(h, copy):
            copy(out=y_sb[h][:], in_=y_bank[h % 4][:])
            nc.sync.dma_start(out=out[h].rearrange("(m r) e -> m (r e)", r=PACK), in_=y_sb[h][:])

        on_scalar, on_vector = nc.scalar.copy, nc.vector.tensor_copy

        nc.scalar.dma_start(out=ka_sb[:], in_=ka)
        nc.scalar.dma_start(out=t_sb[:], in_=t.rearrange("(p j) o -> p (j o)", j=PACK))

        for h in range(4):
            load_keys(h, 1)
        load_keys(4, 2)
        load_queries(0)
        nc.sync.dma_start(
            out=qa_sb[:],
            in_=qa.rearrange("(o m j) z -> o m (j z)", o=1, j=PACK).to_broadcast([PACK, ROWS, PACK]),
        )
        load_values(0)
        load_values(1)
        load_keys(6, 2)
        load_values(2)
        load_queries(1)
        load_values(3)

        for g in range(PAIRS):
            nc.gpsimd.memset(k_scales[g][:].bitcast(U32), 0)
            nc.gpsimd.memset(k_spread[g][:, 0 : 2 * BANK], 0)

        nc.vector.tensor_tensor(
            out=k_weight[:].rearrange("p (x m j) -> p x m j", x=PACK, j=PACK),
            in0=ka_sb[:].rearrange("p (m x) -> p x m", x=PACK).unsqueeze(3).to_broadcast([P, PACK, ROWS, PACK]),
            in1=t_sb[:].unsqueeze(1).unsqueeze(1).to_broadcast([P, PACK, ROWS, PACK]),
            op=ALU.mult,
        )

        for h in range(6):
            square_keys(h)
            weigh_keys(h)
            if h >= 2 and h % 2 == 0:
                quantise_keys(h // 2 - 1)
            if h >= 2 and h % 2 == 1:
                spread_keys(h // 2 - 1)
        nc.vector.tensor_copy(
            out=qa_rep[:].rearrange("p (m j) -> p m j", j=PACK),
            in_=qa_sb[:].unsqueeze(1).to_broadcast([P, ROWS, PACK]),
        )
        quantise_keys(2)

        square_queries(0, 0)
        square_queries(0, 1)
        weigh_queries(0, 0)
        for g in range(2):
            cast_values(2 * g, on_scalar)
            square_queries(0, g + 2)
            cast_values(2 * g + 1, on_vector)
            weigh_queries(0, g + 1)
            quantise_values(g)
        multiply_state(0)
        weigh_queries(0, 3)
        spread_keys(2)

        for i in range(2):
            square_keys(6 + i)
            weigh_keys(6 + i)
            quantise_queries(0, i)
        for h in state_parts[1]:
            cast_values(h, on_scalar)
        quantise_values(2)
        multiply_state(1)
        quantise_keys(3)
        round_state(0)
        quantise_state(0)
        for g in range(2):
            multiply_result(g, 0)
        spread_keys(3)

        for u in range(PACK):
            square_queries(1, u)
        weigh_queries(1, 0)
        for h in state_parts[2]:
            cast_values(h, on_vector)
        weigh_queries(1, 1)
        quantise_values(3)
        multiply_state(2)

        round_state(1)
        for h in range(3):
            store_result(h, on_scalar)
        round_state(2)
        weigh_queries(1, 2)
        weigh_queries(1, 3)
        quantise_state(1)
        quantise_queries(1, 0)
        quantise_queries(1, 1)
        multiply_result(2, 1)
        store_result(3, on_vector)
        quantise_state(2)
        multiply_result(3, 2)
        for h in range(4, H):
            store_result(h, on_vector if h % 2 else on_scalar)
